import numpy as np
import ml_dtypes


def mxq(x, axis, fmt="e4m3"):
    dtype, down = {"e4m3": (ml_dtypes.float8_e4m3fn, 7), "e5m2": (ml_dtypes.float8_e5m2, 14)}[fmt]
    v = np.moveaxis(np.asarray(x, np.float32).astype(ml_dtypes.bfloat16).astype(np.float64), axis, -1)
    blocks = v.reshape(v.shape[:-1] + (-1, 32))
    amax = np.abs(blocks).max(-1, keepdims=True)
    byte = np.maximum(np.where(amax > 0, np.frexp(amax)[1] - 1 + 127, 0) - down, 1)
    scale = np.exp2(byte - 127.0)
    codes = (blocks / scale).astype(np.float32).astype(dtype).astype(np.float64)
    return np.moveaxis((codes * scale).reshape(v.shape), -1, axis)


WIDE = False


def mx_kscale(k):
    if not WIDE:
        return np.ones(k)
    levels = np.array([10, -10, 5, -5, 0])
    if k % 512:
        return np.exp2(np.random.permutation(np.resize(levels, k // 32))).repeat(32)
    a = np.empty((k // 512, 16))
    for p in range(k // 512):
        a[p, :8] = np.random.permutation(np.resize(levels, 8))
        for g in range(8):
            far = levels[np.abs(levels - a[p, g]) >= 10]
            a[p, g + 8] = far[np.random.randint(len(far))]
    return np.exp2(a.ravel()).repeat(32)


def f64(x):
    return np.asarray(x).astype(np.float64)


def striped8(idx):
    return np.concatenate([v.reshape(-1, 16).T for v in idx]).astype(np.uint16)


def unstriped8(offs):
    return np.stack([offs[16 * g:16 * g + 16].T.reshape(-1) for g in range(8)]).astype(np.int64)


E2M1 = np.array([0.0, 0.5, 1.0, 1.5, 2.0, 3.0, 4.0, 6.0, -0.0, -0.5, -1.0, -1.5, -2.0, -3.0, -4.0, -6.0])


def pack_weight(w, fmt):
    k, n = w.shape
    w = f64(np.asarray(w, np.float32).astype(ml_dtypes.bfloat16)).reshape(k // 32, 32, n)
    amax = np.abs(w).max(1)
    if fmt == "e4m3":
        byte = np.frexp(amax)[1] - 1 + 127 - 7
    else:
        mant, ex = np.frexp(amax / 6.0)
        byte = np.where(mant > 0.5, ex, ex - 1) + 127
    byte = np.clip(np.where(amax > 0, byte, 1), 1, 254)
    scaled = (w * np.exp2(127.0 - byte)[:, None, :]).reshape(k, n).astype(np.float32)
    by_word = np.ascontiguousarray(scaled.reshape(k // 512, 128, 4, n).transpose(0, 1, 3, 2))
    if fmt == "e4m3":
        words = by_word.astype(ml_dtypes.float8_e4m3fn).view(np.uint8)
    else:
        c = by_word.astype(ml_dtypes.float4_e2m1fn).view(np.uint8) & 0xF
        words = (c[..., 0::2] | (c[..., 1::2] << 4)).reshape(k // 512, 128, 2 * n)
    return np.ascontiguousarray(words), np.ascontiguousarray(byte.astype(np.uint8).reshape(k // 512, 16, n))


def unpack_weight(words, scales, fmt):
    g, _, n = scales.shape
    words = np.ascontiguousarray(words).reshape(g, 128, n, -1)
    if fmt == "e4m3":
        vals = words.view(ml_dtypes.float8_e4m3fn).astype(np.float64)
    else:
        nib = np.empty((g, 128, n, 4), np.uint8)
        nib[..., 0::2] = words & 0xF
        nib[..., 1::2] = words >> 4
        vals = E2M1[nib]
    vals = vals * np.repeat(np.exp2(scales.astype(np.float64) - 127.0), 8, axis=1)[..., None]
    return vals.transpose(0, 1, 3, 2).reshape(g * 512, n)


def gelu(v):
    return 0.5 * v * (1.0 + np.tanh(np.sqrt(2.0 / np.pi) * (v + 0.044715 * v**3)))


K, M, T, S = 1024, 1024, 1024, 512


def setup_inputs():
    n = np.random.standard_normal
    s = mx_kscale(K)[:, None]
    p_w = pack_weight(n((K, M)) / np.sqrt(K) / s, "e2m1")
    return {
        "x": (n((K, S)) * s).astype(np.float32),
        "w_words": p_w[0],
        "w_scales": p_w[1],
        "b": (0.3 * n(1024)).astype(np.float32),
        "wgo": np.repeat(np.random.uniform(0.5, 2.0, (8, S)), 16, axis=0).astype(np.float32),
        "offs": striped8(np.stack([np.random.permutation(T)[:S] for _ in range(8)])),
    }


def reference(x, w_words, w_scales, b, wgo, offs):
    x_ = mxq(f64(x), 0, "e4m3")
    w_ = unpack_weight(w_words, w_scales, "e2m1")
    y = w_.T @ x_
    place = unstriped8(offs)[np.arange(M) % 128 // 16]
    out = np.zeros((M, T))
    out[np.arange(M)[:, None], place] = f64(wgo)[np.arange(M) % 128] * (gelu(y + f64(b)[:, None]))
    return out

@@ -1,0 +1,160 @@
+from contextlib import ExitStack
+
+import concourse.mybir as mybir
+from concourse.masks import make_identity
+
+K, M, T, S = 1024, 1024, 1024, 512
+FLOPS = 2 * K * M * S
+
+F32 = mybir.dt.float32
+BF16 = mybir.dt.bfloat16
+I32 = mybir.dt.int32
+U32 = mybir.dt.uint32
+U16 = mybir.dt.uint16
+U8 = mybir.dt.uint8
+FP8X4 = mybir.dt.float8_e4m3fn_x4
+FP4X4 = mybir.dt.float4_e2m1fn_x4
+GELU = mybir.ActivationFunctionType.Gelu_apprx_tanh
+MULT = mybir.AluOpType.mult
+
+P = 128
+PASSES = K // 512
+TILES = M // P
+HALF = S // 2
+N_MM = 128
+
+
+def interleave(copy, dst, src):
+    copy(
+        out=dst.rearrange("p (c i) t -> p c t i", i=4),
+        in_=src.rearrange("p t (c i) -> p c t i", i=4),
+    )
+
+
+def tile_list_hscat_gelu_kernel(tc, x, w_words, w_scales, b, wgo, offs, out):
+    nc = tc.nc
+    with ExitStack() as ctx:
+        keep = ctx.enter_context(tc.tile_pool(name="keep", bufs=1))
+        windows = ctx.enter_context(tc.tile_pool(name="windows", bufs=4))
+        vals = ctx.enter_context(tc.tile_pool(name="vals", bufs=4))
+        psum = ctx.enter_context(tc.psum_pool(name="psum", bufs=7))
+        psum_b = ctx.enter_context(tc.psum_pool(name="psum_b", bufs=1))
+
+        offsets = keep.tile([P, S // 16], U16, name="offsets")
+        wgo_sb = keep.tile([P, S], F32, name="wgo_sb")
+        words = keep.tile([P, PASSES, 2 * M], U8, name="words", align_bytes=64)
+        planes = keep.tile([P, PASSES, M], U8, name="planes", align_bytes=64)
+        raw = [[keep.tile([P, 4, HALF], F32, name=f"raw{h}{a}") for a in range(PASSES)] for h in range(2)]
+        grouped = [keep.tile([P, S, 4], BF16, name=f"grouped{a}", align_bytes=64) for a in range(PASSES)]
+        codes = [keep.tile([P, S], U32, name=f"codes{a}", align_bytes=64) for a in range(PASSES)]
+        scales = [keep.tile([P, S], U8, name=f"scales{a}", align_bytes=64) for a in range(PASSES)]
+        warm = keep.tile([P, 1], F32, name="warm")
+        b_rows = keep.tile([P, P], F32, name="b_rows")
+        ident = keep.tile([P, P], F32, name="ident")
+        bias = keep.tile([P, TILES], F32, name="bias")
+
+        x_view = x.rearrange("(a p i) (h j) -> h a p i j", a=PASSES, i=4, h=2)
+        w_view = w_words.bitcast(I32).rearrange("a p n -> p a n")
+        s_view = w_scales.bitcast(I32).rearrange("a q n -> q a n")
+        words_i32 = words[:].rearrange("p a n -> p (a n)").bitcast(I32).rearrange("p (a n) -> p a n", a=PASSES)
+        planes_i32 = planes[:].rearrange("p a n -> p (a n)").bitcast(I32)
+        planes_i32_3 = planes_i32.rearrange("p (a n) -> p a n", a=PASSES)
+
+        nc.vector.memset(planes_i32, 0)
+        nc.gpsimd.memset(b_rows[:], 0.0)
+        nc.sync.dma_start(out=raw[0][0][:], in_=x_view[0, 0])
+        nc.sync.dma_start(out=raw[0][1][:], in_=x_view[0, 1])
+        for q in range(4):
+            nc.scalar.dma_start(out=planes_i32_3[32 * q : 32 * q + 4], in_=s_view[4 * q : 4 * q + 4])
+        nc.scalar.dma_start(out=words_i32[:, :, 0:128], in_=w_view[:, :, 0:128])
+        nc.scalar.dma_start(out=b_rows[0:TILES, :], in_=b.rearrange("(c p) -> c p", p=P))
+        nc.sync.dma_start(offsets[:], offs)
+        nc.sync.dma_start(out=wgo_sb[:], in_=wgo)
+        nc.sync.dma_start(out=words_i32[:, :, 128:512], in_=w_view[:, :, 128:512])
+        nc.sync.dma_start(out=raw[1][0][:], in_=x_view[1, 0])
+        nc.sync.dma_start(out=raw[1][1][:], in_=x_view[1, 1])
+
+        nc.gpsimd.memset(warm[:], 0.0)
+        nc.scalar.activation(out=warm[:], in_=warm[:], func=GELU)
+        make_identity(nc, ident[:])
+
+        wins = []
+
+        def new_window(engine):
+            win = windows.tile([P, T], F32, name="win")
+            engine.memset(win[:], 0.0)
+            wins.append(win)
+
+        for c in range(4):
+            new_window(nc.vector)
+
+        b_t = psum_b.tile([P, P], F32, name="b_t")
+        nc.tensor.transpose(b_t[:], b_rows[:], ident[:])
+        nc.scalar.copy(out=bias[:], in_=b_t[:, 0:TILES])
+
+        def copy_piece(copy, a, j0, width):
+            h = j0 // HALF
+            r0 = j0 - h * HALF
+            interleave(copy, grouped[a][:, j0 : j0 + width, :], raw[h][a][:, :, r0 : r0 + width])
+
+        def quantize_piece(a, j0, width):
+            nc.vector.quantize_mx(
+                out=codes[a][:, j0 : j0 + width].bitcast(FP8X4),
+                scales=scales[a][:, j0 : j0 + width],
+                in_=grouped[a][:, j0 : j0 + width, :].rearrange("p j t -> p (j t)"),
+            )
+
+        def product(c, h):
+            acc = psum.tile([P, HALF], F32, name="acc")
+            for s in range(HALF // N_MM):
+                j0 = h * HALF + s * N_MM
+                for a in range(PASSES):
+                    nc.tensor.matmul_mx(
+                        out=acc[:, s * N_MM : (s + 1) * N_MM],
+                        lhsT=words[:, a, 2 * P * c : 2 * P * (c + 1)].bitcast(FP4X4),
+                        lhsT_scale=planes[:, a, P * c : P * (c + 1)],
+                        rhs=codes[a][:, j0 : j0 + N_MM].bitcast(FP8X4),
+                        rhs_scale=scales[a][:, j0 : j0 + N_MM],
+                        start=(a == 0),
+                        stop=(a == PASSES - 1),
+                    )
+            val = vals.tile([P, HALF], F32, name="val")
+            nc.scalar.activation(out=val[:], in_=acc[:], func=GELU, bias=bias[:, c : c + 1])
+            return val
+
+        def place(c, h, val):
+            nc.vector.tensor_tensor(
+                wins[c][:].indirect(offsets[:, 16 * h : 16 * (h + 1)]),
+                val[:],
+                wgo_sb[:, h * HALF : (h + 1) * HALF],
+                MULT,
+            )
+
+        copy_piece(nc.vector.tensor_copy, 0, 0, 128)
+        copy_piece(nc.vector.tensor_copy, 0, 128, 128)
+        quantize_piece(0, 0, 128)
+        quantize_piece(0, 128, 128)
+        copy_piece(nc.vector.tensor_copy, 1, 0, 128)
+        copy_piece(nc.scalar.copy, 1, 128, 128)
+        quantize_piece(1, 0, 128)
+        quantize_piece(1, 128, 128)
+
+        place(0, 0, product(0, 0))
+        for a in range(PASSES):
+            copy_piece(nc.scalar.copy, a, HALF, HALF)
+        place(1, 0, product(1, 0))
+        for a in range(PASSES):
+            quantize_piece(a, HALF, HALF)
+        place(0, 1, product(0, 1))
+        nc.sync.dma_start(out=out[0:P, :], in_=wins[0][:])
+        place(1, 1, product(1, 1))
+        nc.sync.dma_start(out=out[P : 2 * P, :], in_=wins[1][:])
+        for c in range(2, TILES, 2):
+            if c >= 4:
+                new_window(nc.gpsimd)
+                new_window(nc.gpsimd)
+            place(c, 0, product(c, 0))
+            place(c + 1, 0, product(c + 1, 0))
+            for e in (c, c + 1):
+                place(e, 1, product(e, 1))
+                nc.sync.dma_start(out=out[P * e : P * (e + 1), :], in_=wins[e][:])

@@ -22,6 +22,7 @@ PASSES = K // 512
 TILES = M // P
 HALF = S // 2
 N_MM = 128
+HEAD_WINDOWS = 4
 
 
 def interleave(copy, dst, src):
@@ -35,7 +36,7 @@ def tile_list_hscat_gelu_kernel(tc, x, w_words, w_scales, b, wgo, offs, out):
     nc = tc.nc
     with ExitStack() as ctx:
         keep = ctx.enter_context(tc.tile_pool(name="keep", bufs=1))
-        windows = ctx.enter_context(tc.tile_pool(name="windows", bufs=4))
+        windows = ctx.enter_context(tc.tile_pool(name="windows", bufs=HEAD_WINDOWS))
         vals = ctx.enter_context(tc.tile_pool(name="vals", bufs=4))
         psum = ctx.enter_context(tc.psum_pool(name="psum", bufs=7))
         psum_b = ctx.enter_context(tc.psum_pool(name="psum_b", bufs=1))
@@ -62,31 +63,27 @@ def tile_list_hscat_gelu_kernel(tc, x, w_words, w_scales, b, wgo, offs, out):
 
         nc.vector.memset(planes_i32, 0)
         nc.gpsimd.memset(b_rows[:], 0.0)
+        nc.gpsimd.memset(warm[:], 0.0)
         nc.sync.dma_start(out=raw[0][0][:], in_=x_view[0, 0])
         nc.sync.dma_start(out=raw[0][1][:], in_=x_view[0, 1])
+        nc.sync.dma_start(offsets[:], offs)
+        nc.scalar.dma_start(out=words_i32[:, :, 0:128], in_=w_view[:, :, 0:128])
         for q in range(4):
             nc.scalar.dma_start(out=planes_i32_3[32 * q : 32 * q + 4], in_=s_view[4 * q : 4 * q + 4])
-        nc.scalar.dma_start(out=words_i32[:, :, 0:128], in_=w_view[:, :, 0:128])
-        nc.scalar.dma_start(out=b_rows[0:TILES, :], in_=b.rearrange("(c p) -> c p", p=P))
-        nc.sync.dma_start(offsets[:], offs)
-        nc.sync.dma_start(out=wgo_sb[:], in_=wgo)
+        nc.gpsimd.dma_start(out=b_rows[0:TILES, :], in_=b.rearrange("(c p) -> c p", p=P))
+        nc.gpsimd.dma_start(out=wgo_sb[:], in_=wgo)
         nc.sync.dma_start(out=words_i32[:, :, 128:512], in_=w_view[:, :, 128:512])
         nc.sync.dma_start(out=raw[1][0][:], in_=x_view[1, 0])
         nc.sync.dma_start(out=raw[1][1][:], in_=x_view[1, 1])
 
-        nc.gpsimd.memset(warm[:], 0.0)
         nc.scalar.activation(out=warm[:], in_=warm[:], func=GELU)
         make_identity(nc, ident[:])
 
         wins = []
-
-        def new_window(engine):
+        for c in range(HEAD_WINDOWS):
             win = windows.tile([P, T], F32, name="win")
-            engine.memset(win[:], 0.0)
+            (nc.vector if c < 3 else nc.gpsimd).memset(win[:], 0.0)
             wins.append(win)
-
-        for c in range(4):
-            new_window(nc.vector)
 
         b_t = psum_b.tile([P, P], F32, name="b_t")
         nc.tensor.transpose(b_t[:], b_rows[:], ident[:])
@@ -131,30 +128,33 @@ def tile_list_hscat_gelu_kernel(tc, x, w_words, w_scales, b, wgo, offs, out):
             )
 
         copy_piece(nc.vector.tensor_copy, 0, 0, 128)
-        copy_piece(nc.vector.tensor_copy, 0, 128, 128)
+        copy_piece(nc.scalar.copy, 0, 128, 128)
         quantize_piece(0, 0, 128)
-        quantize_piece(0, 128, 128)
         copy_piece(nc.vector.tensor_copy, 1, 0, 128)
         copy_piece(nc.scalar.copy, 1, 128, 128)
+        quantize_piece(0, 128, 128)
         quantize_piece(1, 0, 128)
         quantize_piece(1, 128, 128)
 
+        def finish(c):
+            place(c, 1, product(c, 1))
+            nc.sync.dma_start(out=out[P * c : P * (c + 1), :], in_=wins[c][:])
+
         place(0, 0, product(0, 0))
-        for a in range(PASSES):
-            copy_piece(nc.scalar.copy, a, HALF, HALF)
         place(1, 0, product(1, 0))
         for a in range(PASSES):
+            copy_piece(nc.scalar.copy, a, HALF, HALF)
             quantize_piece(a, HALF, HALF)
-        place(0, 1, product(0, 1))
-        nc.sync.dma_start(out=out[0:P, :], in_=wins[0][:])
-        place(1, 1, product(1, 1))
-        nc.sync.dma_start(out=out[P : 2 * P, :], in_=wins[1][:])
-        for c in range(2, TILES, 2):
-            if c >= 4:
-                new_window(nc.gpsimd)
-                new_window(nc.gpsimd)
-            place(c, 0, product(c, 0))
-            place(c + 1, 0, product(c + 1, 0))
+        place(2, 0, product(2, 0))
+        place(3, 0, product(3, 0))
+        for c in range(4):
+            finish(c)
+        for c in range(4, TILES, 2):
             for e in (c, c + 1):
-                place(e, 1, product(e, 1))
-                nc.sync.dma_start(out=out[P * e : P * (e + 1), :], in_=wins[e][:])
+                if e >= HEAD_WINDOWS:
+                    win = windows.tile([P, T], F32, name="win")
+                    nc.gpsimd.memset(win[:], 0.0)
+                    wins.append(win)
+                place(e, 0, product(e, 0))
+            for e in (c, c + 1):
+                finish(e)

@@ -22,7 +22,8 @@ PASSES = K // 512
 TILES = M // P
 HALF = S // 2
 N_MM = 128
-HEAD_WINDOWS = 4
+WINDOWS = 5
+EARLY = 2 * P // 2
 
 
 def interleave(copy, dst, src):
@@ -36,19 +37,19 @@ def tile_list_hscat_gelu_kernel(tc, x, w_words, w_scales, b, wgo, offs, out):
     nc = tc.nc
     with ExitStack() as ctx:
         keep = ctx.enter_context(tc.tile_pool(name="keep", bufs=1))
-        windows = ctx.enter_context(tc.tile_pool(name="windows", bufs=HEAD_WINDOWS))
+        windows = ctx.enter_context(tc.tile_pool(name="windows", bufs=WINDOWS))
         vals = ctx.enter_context(tc.tile_pool(name="vals", bufs=4))
         psum = ctx.enter_context(tc.psum_pool(name="psum", bufs=7))
         psum_b = ctx.enter_context(tc.psum_pool(name="psum_b", bufs=1))
 
         offsets = keep.tile([P, S // 16], U16, name="offsets")
-        wgo_sb = keep.tile([P, S], F32, name="wgo_sb")
+        wgo_sb = [keep.tile([P, HALF], F32, name=f"wgo{h}") for h in range(2)]
         words = keep.tile([P, PASSES, 2 * M], U8, name="words", align_bytes=64)
         planes = keep.tile([P, PASSES, M], U8, name="planes", align_bytes=64)
         raw = [[keep.tile([P, 4, HALF], F32, name=f"raw{h}{a}") for a in range(PASSES)] for h in range(2)]
-        grouped = [keep.tile([P, S, 4], BF16, name=f"grouped{a}", align_bytes=64) for a in range(PASSES)]
-        codes = [keep.tile([P, S], U32, name=f"codes{a}", align_bytes=64) for a in range(PASSES)]
-        scales = [keep.tile([P, S], U8, name=f"scales{a}", align_bytes=64) for a in range(PASSES)]
+        grouped = [keep.tile([P, PASSES, HALF, 4], BF16, name=f"grouped{h}", align_bytes=64) for h in range(2)]
+        codes = [keep.tile([P, PASSES, HALF], U32, name=f"codes{h}", align_bytes=64) for h in range(2)]
+        scales = [keep.tile([P, PASSES, HALF], U8, name=f"scales{h}", align_bytes=64) for h in range(2)]
         warm = keep.tile([P, 1], F32, name="warm")
         b_rows = keep.tile([P, P], F32, name="b_rows")
         ident = keep.tile([P, P], F32, name="ident")
@@ -61,100 +62,99 @@ def tile_list_hscat_gelu_kernel(tc, x, w_words, w_scales, b, wgo, offs, out):
         planes_i32 = planes[:].rearrange("p a n -> p (a n)").bitcast(I32)
         planes_i32_3 = planes_i32.rearrange("p (a n) -> p a n", a=PASSES)
 
+        wins = []
+
+        def new_window(engine):
+            win = windows.tile([P, T], F32, name="win")
+            engine.memset(win[:], 0.0)
+            wins.append(win)
+
         nc.vector.memset(planes_i32, 0)
         nc.gpsimd.memset(b_rows[:], 0.0)
-        nc.gpsimd.memset(warm[:], 0.0)
-        nc.sync.dma_start(out=raw[0][0][:], in_=x_view[0, 0])
-        nc.sync.dma_start(out=raw[0][1][:], in_=x_view[0, 1])
         nc.sync.dma_start(offsets[:], offs)
-        nc.scalar.dma_start(out=words_i32[:, :, 0:128], in_=w_view[:, :, 0:128])
+        nc.sync.dma_start(out=raw[0][0][:], in_=x_view[0, 0])
         for q in range(4):
-            nc.scalar.dma_start(out=planes_i32_3[32 * q : 32 * q + 4], in_=s_view[4 * q : 4 * q + 4])
+            nc.sync.dma_start(out=planes_i32_3[32 * q : 32 * q + 4], in_=s_view[4 * q : 4 * q + 4])
+        nc.sync.dma_start(out=raw[0][1][:], in_=x_view[0, 1])
+        nc.sync.dma_start(out=words_i32[:, :, 0:EARLY], in_=w_view[:, :, 0:EARLY])
+        nc.sync.dma_start(out=wgo_sb[0][:], in_=wgo[:, 0:HALF])
         nc.gpsimd.dma_start(out=b_rows[0:TILES, :], in_=b.rearrange("(c p) -> c p", p=P))
-        nc.gpsimd.dma_start(out=wgo_sb[:], in_=wgo)
-        nc.sync.dma_start(out=words_i32[:, :, 128:512], in_=w_view[:, :, 128:512])
+        nc.sync.dma_start(out=words_i32[:, :, EARLY:], in_=w_view[:, :, EARLY:])
         nc.sync.dma_start(out=raw[1][0][:], in_=x_view[1, 0])
         nc.sync.dma_start(out=raw[1][1][:], in_=x_view[1, 1])
+        nc.sync.dma_start(out=wgo_sb[1][:], in_=wgo[:, HALF:S])
 
-        nc.scalar.activation(out=warm[:], in_=warm[:], func=GELU)
         make_identity(nc, ident[:])
-
-        wins = []
-        for c in range(HEAD_WINDOWS):
-            win = windows.tile([P, T], F32, name="win")
-            (nc.vector if c < 3 else nc.gpsimd).memset(win[:], 0.0)
-            wins.append(win)
+        for c in range(3):
+            new_window(nc.vector)
+        new_window(nc.gpsimd)
+        nc.scalar.activation(out=warm[:], in_=wins[0][:, 0:1], func=GELU)
 
         b_t = psum_b.tile([P, P], F32, name="b_t")
         nc.tensor.transpose(b_t[:], b_rows[:], ident[:])
         nc.scalar.copy(out=bias[:], in_=b_t[:, 0:TILES])
 
-        def copy_piece(copy, a, j0, width):
-            h = j0 // HALF
-            r0 = j0 - h * HALF
-            interleave(copy, grouped[a][:, j0 : j0 + width, :], raw[h][a][:, :, r0 : r0 + width])
+        def copy_piece(copy, h, a, j0, j1):
+            interleave(copy, grouped[h][:, a, j0:j1, :], raw[h][a][:, :, j0:j1])
 
-        def quantize_piece(a, j0, width):
+        def quantize_piece(h, a, j0, j1):
             nc.vector.quantize_mx(
-                out=codes[a][:, j0 : j0 + width].bitcast(FP8X4),
-                scales=scales[a][:, j0 : j0 + width],
-                in_=grouped[a][:, j0 : j0 + width, :].rearrange("p j t -> p (j t)"),
+                out=codes[h][:, a, j0:j1].bitcast(FP8X4),
+                scales=scales[h][:, a, j0:j1],
+                in_=grouped[h][:, a, j0:j1, :].rearrange("p j t -> p (j t)"),
             )
 
         def product(c, h):
-            acc = psum.tile([P, HALF], F32, name="acc")
-            for s in range(HALF // N_MM):
-                j0 = h * HALF + s * N_MM
+            val = vals.tile([P, HALF], F32, name="val")
+            for j0 in range(0, HALF, N_MM):
+                j1 = j0 + N_MM
+                acc = psum.tile([P, N_MM], F32, name="acc")
                 for a in range(PASSES):
                     nc.tensor.matmul_mx(
-                        out=acc[:, s * N_MM : (s + 1) * N_MM],
+                        out=acc[:],
                         lhsT=words[:, a, 2 * P * c : 2 * P * (c + 1)].bitcast(FP4X4),
                         lhsT_scale=planes[:, a, P * c : P * (c + 1)],
-                        rhs=codes[a][:, j0 : j0 + N_MM].bitcast(FP8X4),
-                        rhs_scale=scales[a][:, j0 : j0 + N_MM],
+                        rhs=codes[h][:, a, j0:j1].bitcast(FP8X4),
+                        rhs_scale=scales[h][:, a, j0:j1],
                         start=(a == 0),
                         stop=(a == PASSES - 1),
                     )
-            val = vals.tile([P, HALF], F32, name="val")
-            nc.scalar.activation(out=val[:], in_=acc[:], func=GELU, bias=bias[:, c : c + 1])
+                nc.scalar.activation(out=val[:, j0:j1], in_=acc[:], func=GELU, bias=bias[:, c : c + 1])
             return val
 
         def place(c, h, val):
             nc.vector.tensor_tensor(
-                wins[c][:].indirect(offsets[:, 16 * h : 16 * (h + 1)]),
-                val[:],
-                wgo_sb[:, h * HALF : (h + 1) * HALF],
-                MULT,
+                wins[c][:].indirect(offsets[:, 16 * h : 16 * (h + 1)]), val[:], wgo_sb[h][:], MULT
             )
-
-        copy_piece(nc.vector.tensor_copy, 0, 0, 128)
-        copy_piece(nc.scalar.copy, 0, 128, 128)
-        quantize_piece(0, 0, 128)
-        copy_piece(nc.vector.tensor_copy, 1, 0, 128)
-        copy_piece(nc.scalar.copy, 1, 128, 128)
-        quantize_piece(0, 128, 128)
-        quantize_piece(1, 0, 128)
-        quantize_piece(1, 128, 128)
 
         def finish(c):
             place(c, 1, product(c, 1))
             nc.sync.dma_start(out=out[P * c : P * (c + 1), :], in_=wins[c][:])
 
+        for a in range(PASSES):
+            copy_piece(nc.vector.tensor_copy, 0, a, 0, 128)
+            copy_piece(nc.scalar.copy, 0, a, 128, 256)
+            quantize_piece(0, a, 0, 128)
+            quantize_piece(0, a, 128, 256)
+        new_window(nc.vector)
+
         place(0, 0, product(0, 0))
         place(1, 0, product(1, 0))
         for a in range(PASSES):
-            copy_piece(nc.scalar.copy, a, HALF, HALF)
-            quantize_piece(a, HALF, HALF)
+            copy_piece(nc.scalar.copy, 1, a, 0, HALF)
+        nc.vector.quantize_mx(
+            out=codes[1][:].rearrange("p a j -> p (a j)").bitcast(FP8X4),
+            scales=scales[1][:].rearrange("p a j -> p (a j)"),
+            in_=grouped[1][:].rearrange("p a j t -> p (a j t)"),
+        )
         place(2, 0, product(2, 0))
         place(3, 0, product(3, 0))
         for c in range(4):
             finish(c)
         for c in range(4, TILES, 2):
             for e in (c, c + 1):
-                if e >= HEAD_WINDOWS:
-                    win = windows.tile([P, T], F32, name="win")
-                    nc.gpsimd.memset(win[:], 0.0)
-                    wins.append(win)
+                if e >= WINDOWS:
+                    new_window(nc.gpsimd)
                 place(e, 0, product(e, 0))
             for e in (c, c + 1):
                 finish(e)

@@ -22,7 +22,6 @@ PASSES = K // 512
 TILES = M // P
 HALF = S // 2
 N_MM = 128
-WINDOWS = 5
 EARLY = 2 * P // 2
 
 
@@ -37,7 +36,7 @@ def tile_list_hscat_gelu_kernel(tc, x, w_words, w_scales, b, wgo, offs, out):
     nc = tc.nc
     with ExitStack() as ctx:
         keep = ctx.enter_context(tc.tile_pool(name="keep", bufs=1))
-        windows = ctx.enter_context(tc.tile_pool(name="windows", bufs=WINDOWS))
+        windows = ctx.enter_context(tc.tile_pool(name="windows", bufs=TILES))
         vals = ctx.enter_context(tc.tile_pool(name="vals", bufs=4))
         psum = ctx.enter_context(tc.psum_pool(name="psum", bufs=7))
         psum_b = ctx.enter_context(tc.psum_pool(name="psum_b", bufs=1))
@@ -66,28 +65,27 @@ def tile_list_hscat_gelu_kernel(tc, x, w_words, w_scales, b, wgo, offs, out):
 
         def new_window(engine):
             win = windows.tile([P, T], F32, name="win")
-            engine.memset(win[:], 0.0)
+            engine.memset(win[:].bitcast(I32), 0)
             wins.append(win)
 
         nc.vector.memset(planes_i32, 0)
         nc.gpsimd.memset(b_rows[:], 0.0)
+        make_identity(nc, ident[:])
         nc.sync.dma_start(offsets[:], offs)
+        nc.scalar.dma_start(out=b_rows[0:TILES, :], in_=b.rearrange("(c p) -> c p", p=P))
         nc.sync.dma_start(out=raw[0][0][:], in_=x_view[0, 0])
         for q in range(4):
             nc.sync.dma_start(out=planes_i32_3[32 * q : 32 * q + 4], in_=s_view[4 * q : 4 * q + 4])
         nc.sync.dma_start(out=raw[0][1][:], in_=x_view[0, 1])
         nc.sync.dma_start(out=words_i32[:, :, 0:EARLY], in_=w_view[:, :, 0:EARLY])
         nc.sync.dma_start(out=wgo_sb[0][:], in_=wgo[:, 0:HALF])
-        nc.gpsimd.dma_start(out=b_rows[0:TILES, :], in_=b.rearrange("(c p) -> c p", p=P))
         nc.sync.dma_start(out=words_i32[:, :, EARLY:], in_=w_view[:, :, EARLY:])
         nc.sync.dma_start(out=raw[1][0][:], in_=x_view[1, 0])
         nc.sync.dma_start(out=raw[1][1][:], in_=x_view[1, 1])
         nc.sync.dma_start(out=wgo_sb[1][:], in_=wgo[:, HALF:S])
 
-        make_identity(nc, ident[:])
-        for c in range(3):
+        for c in range(6):
             new_window(nc.vector)
-        new_window(nc.gpsimd)
         nc.scalar.activation(out=warm[:], in_=wins[0][:, 0:1], func=GELU)
 
         b_t = psum_b.tile([P, P], F32, name="b_t")
@@ -129,14 +127,19 @@ def tile_list_hscat_gelu_kernel(tc, x, w_words, w_scales, b, wgo, offs, out):
 
         def finish(c):
             place(c, 1, product(c, 1))
-            nc.sync.dma_start(out=out[P * c : P * (c + 1), :], in_=wins[c][:])
+            if c < TILES - 1:
+                nc.sync.dma_start(out=out[P * c : P * (c + 1), :], in_=wins[c][:])
+            else:
+                for queue, t0 in ((nc.sync, 0), (nc.scalar, T // 2)):
+                    queue.dma_start(out=out[P * c : P * (c + 1), t0 : t0 + T // 2], in_=wins[c][:, t0 : t0 + T // 2])
 
         for a in range(PASSES):
             copy_piece(nc.vector.tensor_copy, 0, a, 0, 128)
             copy_piece(nc.scalar.copy, 0, a, 128, 256)
             quantize_piece(0, a, 0, 128)
             quantize_piece(0, a, 128, 256)
-        new_window(nc.vector)
+        for c in range(2):
+            new_window(nc.vector)
 
         place(0, 0, product(0, 0))
         place(1, 0, product(1, 0))
@@ -153,8 +156,6 @@ def tile_list_hscat_gelu_kernel(tc, x, w_words, w_scales, b, wgo, offs, out):
             finish(c)
         for c in range(4, TILES, 2):
             for e in (c, c + 1):
-                if e >= WINDOWS:
-                    new_window(nc.gpsimd)
                 place(e, 0, product(e, 0))
             for e in (c, c + 1):
                 finish(e)

from contextlib import ExitStack

import concourse.mybir as mybir
from concourse.masks import make_identity

K, M, T, S = 1024, 1024, 1024, 512
FLOPS = 2 * K * M * S

F32 = mybir.dt.float32
BF16 = mybir.dt.bfloat16
I32 = mybir.dt.int32
U32 = mybir.dt.uint32
U16 = mybir.dt.uint16
U8 = mybir.dt.uint8
FP8X4 = mybir.dt.float8_e4m3fn_x4
FP4X4 = mybir.dt.float4_e2m1fn_x4
GELU = mybir.ActivationFunctionType.Gelu_apprx_tanh
MULT = mybir.AluOpType.mult

P = 128
PASSES = K // 512
TILES = M // P
HALF = S // 2
N_MM = 128
EARLY = 2 * P // 2


def interleave(copy, dst, src):
    copy(
        out=dst.rearrange("p (c i) t -> p c t i", i=4),
        in_=src.rearrange("p t (c i) -> p c t i", i=4),
    )


def tile_list_hscat_gelu_kernel(tc, x, w_words, w_scales, b, wgo, offs, out):
    nc = tc.nc
    with ExitStack() as ctx:
        keep = ctx.enter_context(tc.tile_pool(name="keep", bufs=1))
        windows = ctx.enter_context(tc.tile_pool(name="windows", bufs=TILES))
        vals = ctx.enter_context(tc.tile_pool(name="vals", bufs=4))
        psum = ctx.enter_context(tc.psum_pool(name="psum", bufs=7))
        psum_b = ctx.enter_context(tc.psum_pool(name="psum_b", bufs=1))

        offsets = keep.tile([P, S // 16], U16, name="offsets")
        wgo_sb = [keep.tile([P, HALF], F32, name=f"wgo{h}") for h in range(2)]
        words = keep.tile([P, PASSES, 2 * M], U8, name="words", align_bytes=64)
        planes = keep.tile([P, PASSES, M], U8, name="planes", align_bytes=64)
        raw = [[keep.tile([P, 4, HALF], F32, name=f"raw{h}{a}") for a in range(PASSES)] for h in range(2)]
        grouped = [keep.tile([P, PASSES, HALF, 4], BF16, name=f"grouped{h}", align_bytes=64) for h in range(2)]
        codes = [keep.tile([P, PASSES, HALF], U32, name=f"codes{h}", align_bytes=64) for h in range(2)]
        scales = [keep.tile([P, PASSES, HALF], U8, name=f"scales{h}", align_bytes=64) for h in range(2)]
        warm = keep.tile([P, 1], F32, name="warm")
        b_rows = keep.tile([P, P], F32, name="b_rows")
        ident = keep.tile([P, P], F32, name="ident")
        bias = keep.tile([P, TILES], F32, name="bias")

        x_view = x.rearrange("(a p i) (h j) -> h a p i j", a=PASSES, i=4, h=2)
        w_view = w_words.bitcast(I32).rearrange("a p n -> p a n")
        s_view = w_scales.bitcast(I32).rearrange("a q n -> q a n")
        words_i32 = words[:].rearrange("p a n -> p (a n)").bitcast(I32).rearrange("p (a n) -> p a n", a=PASSES)
        planes_i32 = planes[:].rearrange("p a n -> p (a n)").bitcast(I32)
        planes_i32_3 = planes_i32.rearrange("p (a n) -> p a n", a=PASSES)

        wins = []

        def new_window(engine):
            win = windows.tile([P, T], F32, name="win")
            engine.memset(win[:].bitcast(I32), 0)
            wins.append(win)

        nc.vector.memset(planes_i32, 0)
        nc.gpsimd.memset(b_rows[:], 0.0)
        make_identity(nc, ident[:])
        nc.sync.dma_start(offsets[:], offs)
        nc.scalar.dma_start(out=b_rows[0:TILES, :], in_=b.rearrange("(c p) -> c p", p=P))
        nc.sync.dma_start(out=raw[0][0][:], in_=x_view[0, 0])
        for q in range(4):
            nc.sync.dma_start(out=planes_i32_3[32 * q : 32 * q + 4], in_=s_view[4 * q : 4 * q + 4])
        nc.sync.dma_start(out=raw[0][1][:], in_=x_view[0, 1])
        nc.sync.dma_start(out=words_i32[:, :, 0:EARLY], in_=w_view[:, :, 0:EARLY])
        nc.sync.dma_start(out=wgo_sb[0][:], in_=wgo[:, 0:HALF])
        nc.sync.dma_start(out=words_i32[:, :, EARLY:], in_=w_view[:, :, EARLY:])
        nc.sync.dma_start(out=raw[1][0][:], in_=x_view[1, 0])
        nc.sync.dma_start(out=raw[1][1][:], in_=x_view[1, 1])
        nc.sync.dma_start(out=wgo_sb[1][:], in_=wgo[:, HALF:S])

        for c in range(6):
            new_window(nc.vector)
        nc.scalar.activation(out=warm[:], in_=wins[0][:, 0:1], func=GELU)

        b_t = psum_b.tile([P, P], F32, name="b_t")
        nc.tensor.transpose(b_t[:], b_rows[:], ident[:])
        nc.scalar.copy(out=bias[:], in_=b_t[:, 0:TILES])

        def copy_piece(copy, h, a, j0, j1):
            interleave(copy, grouped[h][:, a, j0:j1, :], raw[h][a][:, :, j0:j1])

        def quantize_piece(h, a, j0, j1):
            nc.vector.quantize_mx(
                out=codes[h][:, a, j0:j1].bitcast(FP8X4),
                scales=scales[h][:, a, j0:j1],
                in_=grouped[h][:, a, j0:j1, :].rearrange("p j t -> p (j t)"),
            )

        def product(c, h):
            val = vals.tile([P, HALF], F32, name="val")
            for j0 in range(0, HALF, N_MM):
                j1 = j0 + N_MM
                acc = psum.tile([P, N_MM], F32, name="acc")
                for a in range(PASSES):
                    nc.tensor.matmul_mx(
                        out=acc[:],
                        lhsT=words[:, a, 2 * P * c : 2 * P * (c + 1)].bitcast(FP4X4),
                        lhsT_scale=planes[:, a, P * c : P * (c + 1)],
                        rhs=codes[h][:, a, j0:j1].bitcast(FP8X4),
                        rhs_scale=scales[h][:, a, j0:j1],
                        start=(a == 0),
                        stop=(a == PASSES - 1),
                    )
                nc.scalar.activation(out=val[:, j0:j1], in_=acc[:], func=GELU, bias=bias[:, c : c + 1])
            return val

        def place(c, h, val):
            nc.vector.tensor_tensor(
                wins[c][:].indirect(offsets[:, 16 * h : 16 * (h + 1)]), val[:], wgo_sb[h][:], MULT
            )

        def finish(c):
            place(c, 1, product(c, 1))
            if c < TILES - 1:
                nc.sync.dma_start(out=out[P * c : P * (c + 1), :], in_=wins[c][:])
            else:
                for queue, t0 in ((nc.sync, 0), (nc.scalar, T // 2)):
                    queue.dma_start(out=out[P * c : P * (c + 1), t0 : t0 + T // 2], in_=wins[c][:, t0 : t0 + T // 2])

        for a in range(PASSES):
            copy_piece(nc.vector.tensor_copy, 0, a, 0, 128)
            copy_piece(nc.scalar.copy, 0, a, 128, 256)
            quantize_piece(0, a, 0, 128)
            quantize_piece(0, a, 128, 256)
        for c in range(2):
            new_window(nc.vector)

        place(0, 0, product(0, 0))
        place(1, 0, product(1, 0))
        for a in range(PASSES):
            copy_piece(nc.scalar.copy, 1, a, 0, HALF)
        nc.vector.quantize_mx(
            out=codes[1][:].rearrange("p a j -> p (a j)").bitcast(FP8X4),
            scales=scales[1][:].rearrange("p a j -> p (a j)"),
            in_=grouped[1][:].rearrange("p a j t -> p (a j t)"),
        )
        place(2, 0, product(2, 0))
        place(3, 0, product(3, 0))
        for c in range(4):
            finish(c)
        for c in range(4, TILES, 2):
            for e in (c, c + 1):
                place(e, 0, product(e, 0))
            for e in (c, c + 1):
                finish(e)
